import numpy as np
import ml_dtypes


def mxq(x, axis, fmt="e4m3"):
    dtype, down = {"e4m3": (ml_dtypes.float8_e4m3fn, 7), "e5m2": (ml_dtypes.float8_e5m2, 14)}[fmt]
    v = np.moveaxis(np.asarray(x, np.float32).astype(ml_dtypes.bfloat16).astype(np.float64), axis, -1)
    blocks = v.reshape(v.shape[:-1] + (-1, 32))
    amax = np.abs(blocks).max(-1, keepdims=True)
    byte = np.maximum(np.where(amax > 0, np.frexp(amax)[1] - 1 + 127, 0) - down, 1)
    scale = np.exp2(byte - 127.0)
    codes = (blocks / scale).astype(np.float32).astype(dtype).astype(np.float64)
    return np.moveaxis((codes * scale).reshape(v.shape), -1, axis)


WIDE = False


def mx_kscale(k):
    if not WIDE:
        return np.ones(k)
    levels = np.array([10, -10, 5, -5, 0])
    if k % 512:
        return np.exp2(np.random.permutation(np.resize(levels, k // 32))).repeat(32)
    a = np.empty((k // 512, 16))
    for p in range(k // 512):
        a[p, :8] = np.random.permutation(np.resize(levels, 8))
        for g in range(8):
            far = levels[np.abs(levels - a[p, g]) >= 10]
            a[p, g + 8] = far[np.random.randint(len(far))]
    return np.exp2(a.ravel()).repeat(32)


def f64(x):
    return np.asarray(x).astype(np.float64)


def striped(idx):
    return np.tile(idx.reshape(-1, 16).T, (8, 1)).astype(np.uint16)


def unstriped(offs):
    return offs[:16].T.reshape(-1).astype(np.int64)


def striped8(idx):
    return np.concatenate([x.reshape(-1, 16).T for x in idx]).astype(np.uint16)


def runs(offs, k):
    lists = np.stack([offs[16 * r : 16 * r + 16].T.reshape(-1) for r in range(8)]).astype(np.int64)
    return lists[np.arange(k) % 512 // 64]


def pack_weight(w):
    k, n = w.shape
    w = f64(np.asarray(w, np.float32).astype(ml_dtypes.bfloat16)).reshape(k // 32, 32, n)
    amax = np.abs(w).max(1)
    byte = np.clip(np.where(amax > 0, np.frexp(amax)[1] - 1 + 127 - 7, 1), 1, 254)
    scaled = (w * np.exp2(127.0 - byte)[:, None, :]).reshape(k, n).astype(np.float32)
    words = np.ascontiguousarray(scaled.reshape(k // 512, 128, 4, n).transpose(0, 1, 3, 2)).astype(ml_dtypes.float8_e4m3fn).view(np.uint8)
    return words, np.ascontiguousarray(byte.astype(np.uint8).reshape(k // 512, 16, n))


def unpack_weight(words, scales):
    g, p, n, _ = words.shape
    vals = np.ascontiguousarray(words).view(ml_dtypes.float8_e4m3fn).astype(np.float64) * np.repeat(np.exp2(scales.astype(np.float64) - 127.0), 8, axis=1)[..., None]
    return vals.transpose(0, 1, 3, 2).reshape(g * 512, n)

def planes(y):
    n, m = y.shape
    v = y.astype(np.float32).astype(ml_dtypes.bfloat16).astype(np.float64).reshape(n // 32, 32, m)
    top = np.abs(v).max(1)
    byte = np.clip(np.where(top > 0, np.frexp(top)[1] - 1 + 127 - 7, 1), 1, 254)
    codes = (v * np.exp2(127.0 - byte)[:, None, :]).reshape(n, m).astype(np.float32).astype(ml_dtypes.float8_e4m3fn).view(np.uint8)
    words = codes.reshape(n // 512, 128, 4, m).transpose(0, 1, 3, 2)
    return np.ascontiguousarray(words), np.ascontiguousarray(byte.astype(np.uint8).reshape(n // 512, 16, m))


K, T, S, V, H, C = 512, 2048, 512, 256, 512, 512


def setup_inputs():
    n = np.random.standard_normal
    s = mx_kscale(K)[:, None]
    packed_xT = pack_weight(n((K, T)) * s)
    packed_w1 = pack_weight(n((K, H)) / np.sqrt(K) / s)
    perm = np.stack([np.random.permutation(S) for _ in range(8)])
    return {
        "x_words": packed_xT[0],
        "x_scales": packed_xT[1],
        "w1_words": packed_w1[0],
        "w1_scales": packed_w1[1],
        "gs": (np.random.uniform(0.5, 1.5, (K, 1)) / s).astype(np.float32),
        "offs": striped(np.random.permutation(T)[:S]),
        "la": striped8(perm[:, :V]),
        "lb": striped8(perm[:, V:]),
        "cand": striped(np.random.permutation(T)[:C]),
    }


def reference(x_words, x_scales, w1_words, w1_scales, gs, offs, la, lb, cand):
    x_cand = unpack_weight(x_words, x_scales)[:, unstriped(cand)]
    xq = unpack_weight(x_words, x_scales)[:, unstriped(offs)]
    h = unpack_weight(w1_words, w1_scales).T @ xq
    b = h[np.arange(H)[:, None], runs(lb, H)]
    a = h[np.arange(H)[:, None], runs(la, H)]
    mn = 0.5 * (a + b)
    db = np.abs(b - mn)
    d1 = np.zeros((H, S))
    d1[np.arange(H)[:, None], runs(la, H)] = mn
    d2 = d1.copy()
    d2[np.arange(H)[:, None], runs(lb, H)] = db
    z = f64(gs) * d2
    out_0 = 0.0625 * ((x_cand.T @ mxq(z, 0, "e4m3")))
    return (out_0,) + planes(out_0)

@@ -1,0 +1,154 @@
+from contextlib import ExitStack
+
+import concourse.mybir as mybir
+
+K, T, S, V, H, C = 512, 2048, 512, 256, 512, 512
+FLOPS = 2 * K * H * S + 2 * K * C * S
+
+F32 = mybir.dt.float32
+BF16 = mybir.dt.bfloat16
+I32 = mybir.dt.int32
+U32 = mybir.dt.uint32
+U16 = mybir.dt.uint16
+U8 = mybir.dt.uint8
+FP8X4 = mybir.dt.float8_e4m3fn_x4
+ALU = mybir.AluOpType
+ACT = mybir.ActivationFunctionType
+
+P = 128
+PACK = 4
+QUADS = 4
+CHUNK = 128
+N_CHUNKS = S // CHUNK
+VEC_COLS = 128
+
+
+def as_words(dram_bytes):
+    return dram_bytes.rearrange("p n t -> p (n t)").bitcast(I32)
+
+
+def dealt(tile):
+    return tile[:].rearrange("p (t m) -> p m t", t=PACK)
+
+
+def tile_picked_candhaar_none_po_kernel(
+    tc, x_words, x_scales, w1_words, w1_scales, gs, offs, la, lb, cand, out_0, out_1, out_2
+):
+    nc = tc.nc
+    with ExitStack() as ctx:
+        keep = ctx.enter_context(tc.tile_pool(name="keep", bufs=1))
+        psum = ctx.enter_context(tc.psum_pool(name="psum", bufs=1))
+
+        offs_t = keep.tile([P, S // 16], U16, name="offs_t")
+        cand_t = keep.tile([P, C // 16], U16, name="cand_t")
+        la_t = keep.tile([P, V // 16], U16, name="la_t")
+        lb_t = keep.tile([P, V // 16], U16, name="lb_t")
+        xw = keep.tile([P, T], I32, name="xw", align_bytes=64)
+        xs = keep.tile([P, T], U8, name="xs", align_bytes=64)
+        ww = keep.tile([P, H], I32, name="ww", align_bytes=64)
+        ws = keep.tile([P, H], U8, name="ws", align_bytes=64)
+        gs_t = keep.tile([P, PACK], F32, name="gs_t")
+
+        nc.vector.memset(xs[:].bitcast(I32), 0)
+        nc.vector.memset(ws[:].bitcast(I32), 0)
+        for q in range(QUADS):
+            nc.sync.dma_start(out=xs[32 * q : 32 * q + 4, :].bitcast(I32), in_=x_scales[0, 4 * q : 4 * q + 4, :].bitcast(I32))
+        nc.sync.dma_start(offs_t[:], offs)
+        nc.sync.dma_start(cand_t[:], cand)
+        nc.sync.dma_start(la_t[:], la)
+        nc.sync.dma_start(out=xw[:], in_=as_words(x_words[0]))
+        nc.sync.dma_start(out=ww[:], in_=as_words(w1_words[0]))
+        for q in range(QUADS):
+            nc.sync.dma_start(out=ws[32 * q : 32 * q + 4, :].bitcast(I32), in_=w1_scales[0, 4 * q : 4 * q + 4, :].bitcast(I32))
+        nc.sync.dma_start(lb_t[:], lb)
+        nc.sync.dma_start(out=gs_t[:], in_=gs.rearrange("(p t) o -> p (t o)", t=PACK))
+
+        wdw = keep.tile([P, H], U32, name="wdw", align_bytes=64)
+        wds = keep.tile([P, H], U8, name="wds", align_bytes=64)
+        nc.scalar.copy(out=dealt(wdw), in_=ww[:].bitcast(U32).rearrange("p (m t) -> p m t", t=PACK))
+        for t in range(PACK):
+            nc.gpsimd.tensor_copy(out=wds[:, P * t : P * (t + 1)], in_=ws[:, t::PACK])
+
+        xqw = keep.tile([P, S], U32, name="xqw", align_bytes=64)
+        xqs = keep.tile([P, S], U8, name="xqs", align_bytes=64)
+        xcw = keep.tile([P, C], U32, name="xcw", align_bytes=64)
+        xcs = keep.tile([P, C], U8, name="xcs", align_bytes=64)
+        halves = [slice(0, S // 2), slice(S // 2, S)]
+        nc.vector.tensor_copy(xqs[:], xs[:].indirect(offs_t[:]))
+        for half in halves:
+            nc.vector.tensor_copy(xqw[:, half], xw[:].bitcast(U32).indirect(offs_t[:, half.start // 16 : half.stop // 16]))
+        nc.vector.tensor_copy(dealt(xcs), xs[:].indirect(cand_t[:]))
+        nc.vector.tensor_copy(dealt(xcw), xw[:].bitcast(U32).indirect(cand_t[:]))
+
+        a, b, diff, db, placed = [], [], [], [], []
+        for t in range(PACK):
+            cols = slice(P * t, P * (t + 1))
+            win = keep.tile([P, S], F32, name=f"win{t}")
+            for i, part in enumerate(halves if t == 0 else [slice(0, S)]):
+                h = psum.tile([P, part.stop - part.start], F32, name=f"h{t}{i}", tag=f"bank{t + 4 * i}")
+                nc.tensor.matmul_mx(out=h[:], lhsT=wdw[:, cols].bitcast(FP8X4), lhsT_scale=wds[:, cols],
+                                    rhs=xqw[:, part].bitcast(FP8X4), rhs_scale=xqs[:, part], start=True, stop=True)
+                nc.scalar.activation(out=win[:, part], in_=h[:], func=ACT.Copy, scale=0.5)
+            a.append(keep.tile([P, V], F32, name=f"a{t}"))
+            b.append(keep.tile([P, V], F32, name=f"b{t}"))
+            nc.scalar.activation(out=a[t][:], in_=win[:].indirect(la_t[:]), func=ACT.Copy)
+            nc.scalar.activation(out=b[t][:], in_=win[:].indirect(lb_t[:]), func=ACT.Copy)
+            diff.append(keep.tile([P, V], F32, name=f"diff{t}"))
+            db.append(keep.tile([P, V], F32, name=f"db{t}"))
+            placed.append(keep.tile([P, S], F32, name=f"placed{t}"))
+
+        zb = keep.tile([P, S, PACK], BF16, name="zb", align_bytes=64)
+
+        def weave(t, cols):
+            if t >= 2 and cols.start < VEC_COLS:
+                nc.vector.tensor_scalar(out=zb[:, cols, t], in0=placed[t][:, cols], scalar1=gs_t[:, t : t + 1], scalar2=None, op0=ALU.mult)
+            else:
+                nc.scalar.activation(out=zb[:, cols, t], in_=placed[t][:, cols], func=ACT.Copy, scale=gs_t[:, t : t + 1])
+
+        for t in range(PACK):
+            nc.vector.tensor_tensor(placed[t][:].indirect(la_t[:]), a[t][:], b[t][:], ALU.add)
+            nc.vector.tensor_tensor(diff[t][:], b[t][:], a[t][:], ALU.subtract)
+            nc.scalar.activation(out=db[t][:], in_=diff[t][:], func=ACT.Abs)
+        for t in range(PACK):
+            nc.vector.tensor_copy(placed[t][:].indirect(lb_t[:]), db[t][:])
+        weave(0, slice(0, S))
+        weave(1, slice(0, S))
+        weave(2, slice(VEC_COLS, S))
+
+        zw = keep.tile([P, S], U32, name="zw", align_bytes=64)
+        zs = keep.tile([P, S], U8, name="zs", align_bytes=64)
+        ow = keep.tile([P, S], I32, name="ow", align_bytes=64)
+        osc = keep.tile([P, S], U8, name="osc", align_bytes=64)
+        out_rows = out_0.rearrange("(p t) j -> p t j", t=PACK)
+        out_words = as_words(out_1[0])
+        chunks = [slice(CHUNK * c, CHUNK * (c + 1)) for c in range(N_CHUNKS)]
+        for cols in chunks:
+            if cols.start < VEC_COLS:
+                weave(PACK - 2, cols)
+            weave(PACK - 1, cols)
+        banks = []
+        for c, cols in enumerate(chunks):
+            nc.vector.quantize_mx(out=zw[:, cols].bitcast(FP8X4), scales=zs[:, cols],
+                                  in_=zb[:, cols, :].rearrange("p j t -> p (j t)"))
+            bank = psum.tile([P, PACK, CHUNK], F32, name=f"score{c}", tag=f"bank{c}")
+            banks.append(bank)
+            for t in range(PACK):
+                rows = slice(P * t, P * (t + 1))
+                nc.tensor.matmul_mx(out=bank[:, t, :], lhsT=xcw[:, rows].bitcast(FP8X4), lhsT_scale=xcs[:, rows],
+                                    rhs=zw[:, cols].bitcast(FP8X4), rhs_scale=zs[:, cols], start=True, stop=True)
+        for pair in range(N_CHUNKS // 2):
+            ob = keep.tile([P, 2 * CHUNK, PACK], BF16, name=f"ob{pair}", align_bytes=64)
+            for i in range(2):
+                c = 2 * pair + i
+                res = keep.tile([P, PACK, CHUNK], F32, name=f"res{c}")
+                nc.scalar.activation(out=res[:], in_=banks[c][:], func=ACT.Copy, scale=0.0625)
+                nc.sync.dma_start(out=out_rows[:, :, chunks[c]], in_=res[:])
+                nc.vector.tensor_copy(out=ob[:, CHUNK * i : CHUNK * (i + 1), :].rearrange("p (c i) t -> p c t i", i=4),
+                                      in_=res[:].rearrange("p t (c i) -> p c t i", i=4))
+            both = slice(2 * CHUNK * pair, 2 * CHUNK * (pair + 1))
+            nc.vector.quantize_mx(out=ow[:, both].bitcast(FP8X4), scales=osc[:, both],
+                                  in_=ob[:].rearrange("p j t -> p (j t)"))
+            nc.sync.dma_start(out=out_words[:, both], in_=ow[:, both])
+        for q in range(QUADS):
+            eng = nc.sync if q % 2 == 0 else nc.scalar
+            eng.dma_start(out=out_2[0, 4 * q : 4 * q + 4, :].bitcast(I32), in_=osc[32 * q : 32 * q + 4, :].bitcast(I32))

@@ -20,7 +20,8 @@ PACK = 4
 QUADS = 4
 CHUNK = 128
 N_CHUNKS = S // CHUNK
-VEC_COLS = 128
+VEC_CHUNKS = 2
+ORDER = (3, 0, 1, 2)
 
 
 def as_words(dram_bytes):
@@ -57,16 +58,18 @@ def tile_picked_candhaar_none_po_kernel(
         nc.sync.dma_start(cand_t[:], cand)
         nc.sync.dma_start(la_t[:], la)
         nc.sync.dma_start(out=xw[:], in_=as_words(x_words[0]))
-        nc.sync.dma_start(out=ww[:], in_=as_words(w1_words[0]))
         for q in range(QUADS):
             nc.sync.dma_start(out=ws[32 * q : 32 * q + 4, :].bitcast(I32), in_=w1_scales[0, 4 * q : 4 * q + 4, :].bitcast(I32))
+        nc.sync.dma_start(out=ww[:], in_=as_words(w1_words[0]))
         nc.sync.dma_start(lb_t[:], lb)
         nc.sync.dma_start(out=gs_t[:], in_=gs.rearrange("(p t) o -> p (t o)", t=PACK))
 
         wdw = keep.tile([P, H], U32, name="wdw", align_bytes=64)
         wds = keep.tile([P, H], U8, name="wds", align_bytes=64)
-        nc.scalar.copy(out=dealt(wdw), in_=ww[:].bitcast(U32).rearrange("p (m t) -> p m t", t=PACK))
-        for t in range(PACK):
+        ww_by_slot = ww[:].bitcast(U32).rearrange("p (m t) -> p m t", t=PACK)
+        nc.scalar.copy(out=dealt(wdw)[:, :, 3], in_=ww_by_slot[:, :, 3])
+        nc.scalar.copy(out=dealt(wdw)[:, :, :3], in_=ww_by_slot[:, :, :3])
+        for t in ORDER:
             nc.gpsimd.tensor_copy(out=wds[:, P * t : P * (t + 1)], in_=ws[:, t::PACK])
 
         xqw = keep.tile([P, S], U32, name="xqw", align_bytes=64)
@@ -80,40 +83,97 @@ def tile_picked_candhaar_none_po_kernel(
         nc.vector.tensor_copy(dealt(xcs), xs[:].indirect(cand_t[:]))
         nc.vector.tensor_copy(dealt(xcw), xw[:].bitcast(U32).indirect(cand_t[:]))
 
-        a, b, diff, db, placed = [], [], [], [], []
-        for t in range(PACK):
+        a = [keep.tile([P, V], F32, name=f"a{t}") for t in range(PACK)]
+        b = [keep.tile([P, V], F32, name=f"b{t}") for t in range(PACK)]
+        diff = [keep.tile([P, V], F32, name=f"diff{t}") for t in range(PACK)]
+        db = [keep.tile([P, V], F32, name=f"db{t}") for t in range(PACK)]
+        placed = [keep.tile([P, S], F32, name=f"placed{t}") for t in range(PACK)]
+        zb = keep.tile([P, S, PACK], BF16, name="zb", align_bytes=64)
+        zp = keep.tile([P, N_CHUNKS, 2, CHUNK, 2], BF16, name="zp", align_bytes=64)
+
+        def pieces(t):
+            return [slice(0, V // 2), slice(V // 2, V)] if t == ORDER[0] else [slice(0, V)]
+
+        def fetch(t):
             cols = slice(P * t, P * (t + 1))
             win = keep.tile([P, S], F32, name=f"win{t}")
-            for i, part in enumerate(halves if t == 0 else [slice(0, S)]):
+            for i, part in enumerate(halves if t == ORDER[0] else [slice(0, S)]):
                 h = psum.tile([P, part.stop - part.start], F32, name=f"h{t}{i}", tag=f"bank{t + 4 * i}")
                 nc.tensor.matmul_mx(out=h[:], lhsT=wdw[:, cols].bitcast(FP8X4), lhsT_scale=wds[:, cols],
                                     rhs=xqw[:, part].bitcast(FP8X4), rhs_scale=xqs[:, part], start=True, stop=True)
                 nc.scalar.activation(out=win[:, part], in_=h[:], func=ACT.Copy, scale=0.5)
-            a.append(keep.tile([P, V], F32, name=f"a{t}"))
-            b.append(keep.tile([P, V], F32, name=f"b{t}"))
-            nc.scalar.activation(out=a[t][:], in_=win[:].indirect(la_t[:]), func=ACT.Copy)
-            nc.scalar.activation(out=b[t][:], in_=win[:].indirect(lb_t[:]), func=ACT.Copy)
-            diff.append(keep.tile([P, V], F32, name=f"diff{t}"))
-            db.append(keep.tile([P, V], F32, name=f"db{t}"))
-            placed.append(keep.tile([P, S], F32, name=f"placed{t}"))
+            for part in pieces(t):
+                lanes = slice(part.start // 16, part.stop // 16)
+                nc.scalar.activation(out=a[t][:, part], in_=win[:].indirect(la_t[:, lanes]), func=ACT.Copy)
+                if part.stop < V:
+                    nc.vector.tensor_copy(b[t][:, part], win[:].indirect(lb_t[:, lanes]))
+                else:
+                    nc.scalar.activation(out=b[t][:, part], in_=win[:].indirect(lb_t[:, lanes]), func=ACT.Copy)
 
-        zb = keep.tile([P, S, PACK], BF16, name="zb", align_bytes=64)
+        def put_means(t, part=slice(0, V)):
+            lanes = slice(part.start // 16, part.stop // 16)
+            nc.vector.tensor_tensor(placed[t][:].indirect(la_t[:, lanes]), a[t][:, part], b[t][:, part], ALU.add)
 
-        def weave(t, cols):
-            if t >= 2 and cols.start < VEC_COLS:
-                nc.vector.tensor_scalar(out=zb[:, cols, t], in0=placed[t][:, cols], scalar1=gs_t[:, t : t + 1], scalar2=None, op0=ALU.mult)
-            else:
-                nc.scalar.activation(out=zb[:, cols, t], in_=placed[t][:, cols], func=ACT.Copy, scale=gs_t[:, t : t + 1])
-
-        for t in range(PACK):
-            nc.vector.tensor_tensor(placed[t][:].indirect(la_t[:]), a[t][:], b[t][:], ALU.add)
+        def differ(t):
             nc.vector.tensor_tensor(diff[t][:], b[t][:], a[t][:], ALU.subtract)
+
+        def size(t):
             nc.scalar.activation(out=db[t][:], in_=diff[t][:], func=ACT.Abs)
-        for t in range(PACK):
+
+        def put_details(t):
             nc.vector.tensor_copy(placed[t][:].indirect(lb_t[:]), db[t][:])
-        weave(0, slice(0, S))
-        weave(1, slice(0, S))
-        weave(2, slice(VEC_COLS, S))
+
+        def pair_up(t, c0, c1, on_vector=False):
+            dst = zp[:, c0:c1, t // 2, :, t % 2]
+            src = placed[t][:, CHUNK * c0 : CHUNK * c1].rearrange("p (c j) -> p c j", j=CHUNK)
+            if on_vector:
+                nc.vector.tensor_scalar(out=dst, in0=src, scalar1=gs_t[:, t : t + 1], scalar2=None, op0=ALU.mult)
+            else:
+                nc.scalar.activation(out=dst, in_=src, func=ACT.Copy, scale=gs_t[:, t : t + 1])
+
+        def direct(t, on_vector=False):
+            if on_vector:
+                nc.vector.tensor_scalar(out=zb[:, :CHUNK, t], in0=placed[t][:, :CHUNK], scalar1=gs_t[:, t : t + 1], scalar2=None, op0=ALU.mult)
+            else:
+                nc.scalar.activation(out=zb[:, :CHUNK, t], in_=placed[t][:, :CHUNK], func=ACT.Copy, scale=gs_t[:, t : t + 1])
+
+        def weave(c0, c1, on_vector=False):
+            word = I32 if on_vector else U32
+            dst = zb[:, CHUNK * c0 : CHUNK * c1, :].bitcast(word).rearrange("p (c j) w -> p c j w", j=CHUNK)
+            src = zp[:, c0:c1].rearrange("p c w j e -> p c w (j e)").bitcast(word).rearrange("p c w j -> p c j w")
+            if on_vector:
+                nc.vector.tensor_copy(out=dst, in_=src)
+            else:
+                nc.scalar.copy(out=dst, in_=src)
+
+        t0, t1, t2, t3 = ORDER
+        fetch(t0)
+        put_means(t0, pieces(t0)[0])
+        differ(t0)
+        size(t0)
+        put_means(t0, pieces(t0)[1])
+        put_details(t0)
+        fetch(t1)
+        put_means(t1)
+        differ(t1)
+        fetch(t2)
+        size(t1)
+        put_means(t2)
+        differ(t2)
+        fetch(t3)
+        direct(t0)
+        pair_up(t0, 1, N_CHUNKS)
+        size(t2)
+        put_details(t1)
+        put_means(t3)
+        differ(t3)
+        direct(t1)
+        pair_up(t1, 1, N_CHUNKS)
+        size(t3)
+        put_details(t2)
+        put_details(t3)
+        direct(t2)
+        pair_up(t2, 1, N_CHUNKS)
 
         zw = keep.tile([P, S], U32, name="zw", align_bytes=64)
         zs = keep.tile([P, S], U8, name="zs", align_bytes=64)
@@ -122,12 +182,16 @@ def tile_picked_candhaar_none_po_kernel(
         out_rows = out_0.rearrange("(p t) j -> p t j", t=PACK)
         out_words = as_words(out_1[0])
         chunks = [slice(CHUNK * c, CHUNK * (c + 1)) for c in range(N_CHUNKS)]
-        for cols in chunks:
-            if cols.start < VEC_COLS:
-                weave(PACK - 2, cols)
-            weave(PACK - 1, cols)
+        direct(t3, on_vector=True)
+        for c in range(1, VEC_CHUNKS):
+            pair_up(t3, c, c + 1, on_vector=True)
+        pair_up(t3, VEC_CHUNKS, N_CHUNKS)
+        for c in range(VEC_CHUNKS, N_CHUNKS):
+            weave(c, c + 1)
         banks = []
         for c, cols in enumerate(chunks):
+            if 0 < c < VEC_CHUNKS:
+                weave(c, c + 1, on_vector=True)
             nc.vector.quantize_mx(out=zw[:, cols].bitcast(FP8X4), scales=zs[:, cols],
                                   in_=zb[:, cols, :].rearrange("p j t -> p (j t)"))
             bank = psum.tile([P, PACK, CHUNK], F32, name=f"score{c}", tag=f"bank{c}")
@@ -141,10 +205,10 @@ def tile_picked_candhaar_none_po_kernel(
             for i in range(2):
                 c = 2 * pair + i
                 res = keep.tile([P, PACK, CHUNK], F32, name=f"res{c}")
+                ob_c = ob[:, CHUNK * i : CHUNK * (i + 1), :].rearrange("p (c i) t -> p c t i", i=4)
                 nc.scalar.activation(out=res[:], in_=banks[c][:], func=ACT.Copy, scale=0.0625)
                 nc.sync.dma_start(out=out_rows[:, :, chunks[c]], in_=res[:])
-                nc.vector.tensor_copy(out=ob[:, CHUNK * i : CHUNK * (i + 1), :].rearrange("p (c i) t -> p c t i", i=4),
-                                      in_=res[:].rearrange("p t (c i) -> p c t i", i=4))
+                nc.vector.tensor_copy(out=ob_c, in_=res[:].rearrange("p t (c i) -> p c t i", i=4))
             both = slice(2 * CHUNK * pair, 2 * CHUNK * (pair + 1))
             nc.vector.quantize_mx(out=ow[:, both].bitcast(FP8X4), scales=osc[:, both],
                                   in_=ob[:].rearrange("p j t -> p (j t)"))

@@ -20,7 +20,7 @@ PACK = 4
 QUADS = 4
 CHUNK = 128
 N_CHUNKS = S // CHUNK
-VEC_CHUNKS = 2
+VEC_CHUNKS = 3
 ORDER = (3, 0, 1, 2)
 
 
@@ -53,13 +53,13 @@ def tile_picked_candhaar_none_po_kernel(
         nc.vector.memset(xs[:].bitcast(I32), 0)
         nc.vector.memset(ws[:].bitcast(I32), 0)
         for q in range(QUADS):
-            nc.sync.dma_start(out=xs[32 * q : 32 * q + 4, :].bitcast(I32), in_=x_scales[0, 4 * q : 4 * q + 4, :].bitcast(I32))
+            nc.sync.dma_start(out=xs[q::32, :].bitcast(I32), in_=x_scales[0, q::4, :].bitcast(I32))
         nc.sync.dma_start(offs_t[:], offs)
         nc.sync.dma_start(cand_t[:], cand)
         nc.sync.dma_start(la_t[:], la)
         nc.sync.dma_start(out=xw[:], in_=as_words(x_words[0]))
         for q in range(QUADS):
-            nc.sync.dma_start(out=ws[32 * q : 32 * q + 4, :].bitcast(I32), in_=w1_scales[0, 4 * q : 4 * q + 4, :].bitcast(I32))
+            nc.sync.dma_start(out=ws[q::32, :].bitcast(I32), in_=w1_scales[0, q::4, :].bitcast(I32))
         nc.sync.dma_start(out=ww[:], in_=as_words(w1_words[0]))
         nc.sync.dma_start(lb_t[:], lb)
         nc.sync.dma_start(out=gs_t[:], in_=gs.rearrange("(p t) o -> p (t o)", t=PACK))
@@ -115,7 +115,11 @@ def tile_picked_candhaar_none_po_kernel(
             nc.vector.tensor_tensor(placed[t][:].indirect(la_t[:, lanes]), a[t][:, part], b[t][:, part], ALU.add)
 
         def differ(t):
-            nc.vector.tensor_tensor(diff[t][:], b[t][:], a[t][:], ALU.subtract)
+            if t in ORDER[:2]:
+                nc.vector.tensor_tensor(diff[t][:], b[t][:], a[t][:], ALU.subtract)
+            else:
+                diff[t] = b[t]
+                nc.gpsimd.tensor_tensor(b[t][:], b[t][:], a[t][:], ALU.subtract)
 
         def size(t):
             nc.scalar.activation(out=db[t][:], in_=diff[t][:], func=ACT.Abs)
@@ -183,8 +187,6 @@ def tile_picked_candhaar_none_po_kernel(
         out_words = as_words(out_1[0])
         chunks = [slice(CHUNK * c, CHUNK * (c + 1)) for c in range(N_CHUNKS)]
         direct(t3, on_vector=True)
-        for c in range(1, VEC_CHUNKS):
-            pair_up(t3, c, c + 1, on_vector=True)
         pair_up(t3, VEC_CHUNKS, N_CHUNKS)
         for c in range(VEC_CHUNKS, N_CHUNKS):
             weave(c, c + 1)
@@ -192,6 +194,8 @@ def tile_picked_candhaar_none_po_kernel(
         for c, cols in enumerate(chunks):
             if 0 < c < VEC_CHUNKS:
                 weave(c, c + 1, on_vector=True)
+            if c + 1 < VEC_CHUNKS:
+                pair_up(t3, c + 1, c + 2, on_vector=True)
             nc.vector.quantize_mx(out=zw[:, cols].bitcast(FP8X4), scales=zs[:, cols],
                                   in_=zb[:, cols, :].rearrange("p j t -> p (j t)"))
             bank = psum.tile([P, PACK, CHUNK], F32, name=f"score{c}", tag=f"bank{c}")
@@ -206,13 +210,16 @@ def tile_picked_candhaar_none_po_kernel(
                 c = 2 * pair + i
                 res = keep.tile([P, PACK, CHUNK], F32, name=f"res{c}")
                 ob_c = ob[:, CHUNK * i : CHUNK * (i + 1), :].rearrange("p (c i) t -> p c t i", i=4)
+                if c == N_CHUNKS - 1:
+                    nc.scalar.activation(out=ob_c, in_=banks[c][:].rearrange("p t (c i) -> p c t i", i=4), func=ACT.Copy, scale=0.0625)
                 nc.scalar.activation(out=res[:], in_=banks[c][:], func=ACT.Copy, scale=0.0625)
                 nc.sync.dma_start(out=out_rows[:, :, chunks[c]], in_=res[:])
-                nc.vector.tensor_copy(out=ob_c, in_=res[:].rearrange("p t (c i) -> p c t i", i=4))
+                if c < N_CHUNKS - 1:
+                    nc.vector.tensor_copy(out=ob_c, in_=res[:].rearrange("p t (c i) -> p c t i", i=4))
             both = slice(2 * CHUNK * pair, 2 * CHUNK * (pair + 1))
             nc.vector.quantize_mx(out=ow[:, both].bitcast(FP8X4), scales=osc[:, both],
                                   in_=ob[:].rearrange("p j t -> p (j t)"))
             nc.sync.dma_start(out=out_words[:, both], in_=ow[:, both])
         for q in range(QUADS):
             eng = nc.sync if q % 2 == 0 else nc.scalar
-            eng.dma_start(out=out_2[0, 4 * q : 4 * q + 4, :].bitcast(I32), in_=osc[32 * q : 32 * q + 4, :].bitcast(I32))
+            eng.dma_start(out=out_2[0, q::4, :].bitcast(I32), in_=osc[q::32, :].bitcast(I32))

@@ -16,11 +16,13 @@ ALU = mybir.AluOpType
 ACT = mybir.ActivationFunctionType
 
 P = 128
-PACK = 4
-QUADS = 4
+SLOTS = 4
+QUADRANT = 32
+SCALE_ROWS = 4
+GROUP = 16
 CHUNK = 128
 N_CHUNKS = S // CHUNK
-VEC_CHUNKS = 3
+VECTOR_CHUNKS = 3
 ORDER = (3, 0, 1, 2)
 
 
@@ -29,197 +31,203 @@ def as_words(dram_bytes):
 
 
 def dealt(tile):
-    return tile[:].rearrange("p (t m) -> p m t", t=PACK)
+    return tile[:].rearrange("p (t m) -> p m t", t=SLOTS)
+
+
+def list_columns(entries):
+    return slice(entries.start // GROUP, entries.stop // GROUP)
+
+
+def in_halves(n):
+    return [slice(0, n // 2), slice(n // 2, n)]
 
 
 def tile_picked_candhaar_none_po_kernel(
     tc, x_words, x_scales, w1_words, w1_scales, gs, offs, la, lb, cand, out_0, out_1, out_2
 ):
     nc = tc.nc
+    first, second, third, last = ORDER
     with ExitStack() as ctx:
         keep = ctx.enter_context(tc.tile_pool(name="keep", bufs=1))
         psum = ctx.enter_context(tc.psum_pool(name="psum", bufs=1))
 
-        offs_t = keep.tile([P, S // 16], U16, name="offs_t")
-        cand_t = keep.tile([P, C // 16], U16, name="cand_t")
-        la_t = keep.tile([P, V // 16], U16, name="la_t")
-        lb_t = keep.tile([P, V // 16], U16, name="lb_t")
-        xw = keep.tile([P, T], I32, name="xw", align_bytes=64)
-        xs = keep.tile([P, T], U8, name="xs", align_bytes=64)
-        ww = keep.tile([P, H], I32, name="ww", align_bytes=64)
-        ws = keep.tile([P, H], U8, name="ws", align_bytes=64)
-        gs_t = keep.tile([P, PACK], F32, name="gs_t")
+        offs_t = keep.tile([P, S // GROUP], U16, name="offs_t")
+        cand_t = keep.tile([P, C // GROUP], U16, name="cand_t")
+        la_t = keep.tile([P, V // GROUP], U16, name="la_t")
+        lb_t = keep.tile([P, V // GROUP], U16, name="lb_t")
+        x_w = keep.tile([P, T], I32, name="x_w", align_bytes=64)
+        x_s = keep.tile([P, T], U8, name="x_s", align_bytes=64)
+        w1_w = keep.tile([P, H], I32, name="w1_w", align_bytes=64)
+        w1_s = keep.tile([P, H], U8, name="w1_s", align_bytes=64)
+        gs_t = keep.tile([P, SLOTS], F32, name="gs_t")
 
-        nc.vector.memset(xs[:].bitcast(I32), 0)
-        nc.vector.memset(ws[:].bitcast(I32), 0)
-        for q in range(QUADS):
-            nc.sync.dma_start(out=xs[q::32, :].bitcast(I32), in_=x_scales[0, q::4, :].bitcast(I32))
+        nc.vector.memset(x_s[:].bitcast(I32), 0)
+        nc.vector.memset(w1_s[:].bitcast(I32), 0)
+        for r in range(SCALE_ROWS):
+            nc.sync.dma_start(out=x_s[r::QUADRANT, :].bitcast(I32), in_=x_scales[0, r::SCALE_ROWS, :].bitcast(I32))
         nc.sync.dma_start(offs_t[:], offs)
         nc.sync.dma_start(cand_t[:], cand)
         nc.sync.dma_start(la_t[:], la)
-        nc.sync.dma_start(out=xw[:], in_=as_words(x_words[0]))
-        for q in range(QUADS):
-            nc.sync.dma_start(out=ws[q::32, :].bitcast(I32), in_=w1_scales[0, q::4, :].bitcast(I32))
-        nc.sync.dma_start(out=ww[:], in_=as_words(w1_words[0]))
+        nc.sync.dma_start(out=x_w[:], in_=as_words(x_words[0]))
+        for r in range(SCALE_ROWS):
+            nc.sync.dma_start(out=w1_s[r::QUADRANT, :].bitcast(I32), in_=w1_scales[0, r::SCALE_ROWS, :].bitcast(I32))
+        nc.sync.dma_start(out=w1_w[:], in_=as_words(w1_words[0]))
         nc.sync.dma_start(lb_t[:], lb)
-        nc.sync.dma_start(out=gs_t[:], in_=gs.rearrange("(p t) o -> p (t o)", t=PACK))
+        nc.sync.dma_start(out=gs_t[:], in_=gs.rearrange("(p t) o -> p (t o)", t=SLOTS))
 
-        wdw = keep.tile([P, H], U32, name="wdw", align_bytes=64)
-        wds = keep.tile([P, H], U8, name="wds", align_bytes=64)
-        ww_by_slot = ww[:].bitcast(U32).rearrange("p (m t) -> p m t", t=PACK)
-        nc.scalar.copy(out=dealt(wdw)[:, :, 3], in_=ww_by_slot[:, :, 3])
-        nc.scalar.copy(out=dealt(wdw)[:, :, :3], in_=ww_by_slot[:, :, :3])
+        w1_dealt_w = keep.tile([P, H], U32, name="w1_dealt_w", align_bytes=64)
+        w1_dealt_s = keep.tile([P, H], U8, name="w1_dealt_s", align_bytes=64)
+        w1_w_by_slot = w1_w[:].bitcast(U32).rearrange("p (m t) -> p m t", t=SLOTS)
+        nc.scalar.copy(out=dealt(w1_dealt_w)[:, :, first], in_=w1_w_by_slot[:, :, first])
+        nc.scalar.copy(out=dealt(w1_dealt_w)[:, :, :first], in_=w1_w_by_slot[:, :, :first])
         for t in ORDER:
-            nc.gpsimd.tensor_copy(out=wds[:, P * t : P * (t + 1)], in_=ws[:, t::PACK])
+            nc.gpsimd.tensor_copy(out=w1_dealt_s[:, P * t : P * (t + 1)], in_=w1_s[:, t::SLOTS])
 
-        xqw = keep.tile([P, S], U32, name="xqw", align_bytes=64)
-        xqs = keep.tile([P, S], U8, name="xqs", align_bytes=64)
-        xcw = keep.tile([P, C], U32, name="xcw", align_bytes=64)
-        xcs = keep.tile([P, C], U8, name="xcs", align_bytes=64)
-        halves = [slice(0, S // 2), slice(S // 2, S)]
-        nc.vector.tensor_copy(xqs[:], xs[:].indirect(offs_t[:]))
-        for half in halves:
-            nc.vector.tensor_copy(xqw[:, half], xw[:].bitcast(U32).indirect(offs_t[:, half.start // 16 : half.stop // 16]))
-        nc.vector.tensor_copy(dealt(xcs), xs[:].indirect(cand_t[:]))
-        nc.vector.tensor_copy(dealt(xcw), xw[:].bitcast(U32).indirect(cand_t[:]))
+        tok_w = keep.tile([P, S], U32, name="tok_w", align_bytes=64)
+        tok_s = keep.tile([P, S], U8, name="tok_s", align_bytes=64)
+        cand_w = keep.tile([P, C], U32, name="cand_w", align_bytes=64)
+        cand_s = keep.tile([P, C], U8, name="cand_s", align_bytes=64)
+        nc.vector.tensor_copy(tok_s[:], x_s[:].indirect(offs_t[:]))
+        for half in in_halves(S):
+            nc.vector.tensor_copy(tok_w[:, half], x_w[:].bitcast(U32).indirect(offs_t[:, list_columns(half)]))
+        nc.vector.tensor_copy(dealt(cand_s), x_s[:].indirect(cand_t[:]))
+        nc.vector.tensor_copy(dealt(cand_w), x_w[:].bitcast(U32).indirect(cand_t[:]))
 
-        a = [keep.tile([P, V], F32, name=f"a{t}") for t in range(PACK)]
-        b = [keep.tile([P, V], F32, name=f"b{t}") for t in range(PACK)]
-        diff = [keep.tile([P, V], F32, name=f"diff{t}") for t in range(PACK)]
-        db = [keep.tile([P, V], F32, name=f"db{t}") for t in range(PACK)]
-        placed = [keep.tile([P, S], F32, name=f"placed{t}") for t in range(PACK)]
-        zb = keep.tile([P, S, PACK], BF16, name="zb", align_bytes=64)
-        zp = keep.tile([P, N_CHUNKS, 2, CHUNK, 2], BF16, name="zp", align_bytes=64)
-
-        def pieces(t):
-            return [slice(0, V // 2), slice(V // 2, V)] if t == ORDER[0] else [slice(0, V)]
+        a = [keep.tile([P, V], F32, name=f"a{t}") for t in range(SLOTS)]
+        b = [keep.tile([P, V], F32, name=f"b{t}") for t in range(SLOTS)]
+        db = [keep.tile([P, V], F32, name=f"db{t}") for t in range(SLOTS)]
+        d2 = [keep.tile([P, S], F32, name=f"d2_{t}") for t in range(SLOTS)]
+        z_bf = keep.tile([P, S, SLOTS], BF16, name="z_bf", align_bytes=64)
+        z_pairs = keep.tile([P, N_CHUNKS - 1, 2, CHUNK, 2], BF16, name="z_pairs", align_bytes=64)
+        diff = {}
 
         def fetch(t):
             cols = slice(P * t, P * (t + 1))
-            win = keep.tile([P, S], F32, name=f"win{t}")
-            for i, part in enumerate(halves if t == ORDER[0] else [slice(0, S)]):
-                h = psum.tile([P, part.stop - part.start], F32, name=f"h{t}{i}", tag=f"bank{t + 4 * i}")
-                nc.tensor.matmul_mx(out=h[:], lhsT=wdw[:, cols].bitcast(FP8X4), lhsT_scale=wds[:, cols],
-                                    rhs=xqw[:, part].bitcast(FP8X4), rhs_scale=xqs[:, part], start=True, stop=True)
-                nc.scalar.activation(out=win[:, part], in_=h[:], func=ACT.Copy, scale=0.5)
-            for part in pieces(t):
-                lanes = slice(part.start // 16, part.stop // 16)
-                nc.scalar.activation(out=a[t][:, part], in_=win[:].indirect(la_t[:, lanes]), func=ACT.Copy)
-                if part.stop < V:
-                    nc.vector.tensor_copy(b[t][:, part], win[:].indirect(lb_t[:, lanes]))
+            half_h = keep.tile([P, S], F32, name=f"half_h{t}")
+            for i, toks in enumerate(in_halves(S) if t == first else [slice(0, S)]):
+                h = psum.tile([P, toks.stop - toks.start], F32, name=f"h{t}{i}", tag=f"bank{t + SLOTS * i}")
+                nc.tensor.matmul_mx(out=h[:], lhsT=w1_dealt_w[:, cols].bitcast(FP8X4), lhsT_scale=w1_dealt_s[:, cols],
+                                    rhs=tok_w[:, toks].bitcast(FP8X4), rhs_scale=tok_s[:, toks], start=True, stop=True)
+                nc.scalar.activation(out=half_h[:, toks], in_=h[:], func=ACT.Copy, scale=0.5)
+            for pairs in in_halves(V) if t == first else [slice(0, V)]:
+                at_la = half_h[:].indirect(la_t[:, list_columns(pairs)])
+                at_lb = half_h[:].indirect(lb_t[:, list_columns(pairs)])
+                nc.scalar.activation(out=a[t][:, pairs], in_=at_la, func=ACT.Copy)
+                if pairs.stop < V:
+                    nc.vector.tensor_copy(b[t][:, pairs], at_lb)
                 else:
-                    nc.scalar.activation(out=b[t][:, part], in_=win[:].indirect(lb_t[:, lanes]), func=ACT.Copy)
+                    nc.scalar.activation(out=b[t][:, pairs], in_=at_lb, func=ACT.Copy)
 
-        def put_means(t, part=slice(0, V)):
-            lanes = slice(part.start // 16, part.stop // 16)
-            nc.vector.tensor_tensor(placed[t][:].indirect(la_t[:, lanes]), a[t][:, part], b[t][:, part], ALU.add)
+        def put_means(t, pairs=slice(0, V)):
+            nc.vector.tensor_tensor(d2[t][:].indirect(la_t[:, list_columns(pairs)]), a[t][:, pairs], b[t][:, pairs], ALU.add)
 
-        def differ(t):
-            if t in ORDER[:2]:
+        def subtract(t):
+            if t in (first, second):
+                diff[t] = keep.tile([P, V], F32, name=f"diff{t}")
                 nc.vector.tensor_tensor(diff[t][:], b[t][:], a[t][:], ALU.subtract)
             else:
                 diff[t] = b[t]
-                nc.gpsimd.tensor_tensor(b[t][:], b[t][:], a[t][:], ALU.subtract)
+                nc.gpsimd.tensor_tensor(diff[t][:], b[t][:], a[t][:], ALU.subtract)
 
-        def size(t):
+        def take_size(t):
             nc.scalar.activation(out=db[t][:], in_=diff[t][:], func=ACT.Abs)
 
-        def put_details(t):
-            nc.vector.tensor_copy(placed[t][:].indirect(lb_t[:]), db[t][:])
+        def put_sizes(t):
+            nc.vector.tensor_copy(d2[t][:].indirect(lb_t[:]), db[t][:])
 
-        def pair_up(t, c0, c1, on_vector=False):
-            dst = zp[:, c0:c1, t // 2, :, t % 2]
-            src = placed[t][:, CHUNK * c0 : CHUNK * c1].rearrange("p (c j) -> p c j", j=CHUNK)
+        def times_gs(dst, src, t, on_vector):
             if on_vector:
                 nc.vector.tensor_scalar(out=dst, in0=src, scalar1=gs_t[:, t : t + 1], scalar2=None, op0=ALU.mult)
             else:
                 nc.scalar.activation(out=dst, in_=src, func=ACT.Copy, scale=gs_t[:, t : t + 1])
 
-        def direct(t, on_vector=False):
-            if on_vector:
-                nc.vector.tensor_scalar(out=zb[:, :CHUNK, t], in0=placed[t][:, :CHUNK], scalar1=gs_t[:, t : t + 1], scalar2=None, op0=ALU.mult)
-            else:
-                nc.scalar.activation(out=zb[:, :CHUNK, t], in_=placed[t][:, :CHUNK], func=ACT.Copy, scale=gs_t[:, t : t + 1])
+        def round_chunk_0(t, on_vector=False):
+            times_gs(z_bf[:, :CHUNK, t], d2[t][:, :CHUNK], t, on_vector)
 
-        def weave(c0, c1, on_vector=False):
+        def round_to_pairs(t, c0, c1, on_vector=False):
+            src = d2[t][:, CHUNK * c0 : CHUNK * c1].rearrange("p (c j) -> p c j", j=CHUNK)
+            times_gs(z_pairs[:, c0 - 1 : c1 - 1, t // 2, :, t % 2], src, t, on_vector)
+
+        def join_pairs(c, on_vector=False):
             word = I32 if on_vector else U32
-            dst = zb[:, CHUNK * c0 : CHUNK * c1, :].bitcast(word).rearrange("p (c j) w -> p c j w", j=CHUNK)
-            src = zp[:, c0:c1].rearrange("p c w j e -> p c w (j e)").bitcast(word).rearrange("p c w j -> p c j w")
+            dst = z_bf[:, CHUNK * c : CHUNK * (c + 1), :].bitcast(word)
+            src = z_pairs[:, c - 1].rearrange("p w j e -> p w (j e)").bitcast(word).rearrange("p w j -> p j w")
             if on_vector:
                 nc.vector.tensor_copy(out=dst, in_=src)
             else:
                 nc.scalar.copy(out=dst, in_=src)
 
-        t0, t1, t2, t3 = ORDER
-        fetch(t0)
-        put_means(t0, pieces(t0)[0])
-        differ(t0)
-        size(t0)
-        put_means(t0, pieces(t0)[1])
-        put_details(t0)
-        fetch(t1)
-        put_means(t1)
-        differ(t1)
-        fetch(t2)
-        size(t1)
-        put_means(t2)
-        differ(t2)
-        fetch(t3)
-        direct(t0)
-        pair_up(t0, 1, N_CHUNKS)
-        size(t2)
-        put_details(t1)
-        put_means(t3)
-        differ(t3)
-        direct(t1)
-        pair_up(t1, 1, N_CHUNKS)
-        size(t3)
-        put_details(t2)
-        put_details(t3)
-        direct(t2)
-        pair_up(t2, 1, N_CHUNKS)
+        fetch(first)
+        put_means(first, in_halves(V)[0])
+        subtract(first)
+        take_size(first)
+        put_means(first, in_halves(V)[1])
+        put_sizes(first)
+        fetch(second)
+        put_means(second)
+        subtract(second)
+        fetch(third)
+        take_size(second)
+        put_means(third)
+        subtract(third)
+        fetch(last)
+        round_chunk_0(first)
+        round_to_pairs(first, 1, N_CHUNKS)
+        take_size(third)
+        put_sizes(second)
+        put_means(last)
+        subtract(last)
+        round_chunk_0(second)
+        round_to_pairs(second, 1, N_CHUNKS)
+        take_size(last)
+        put_sizes(third)
+        put_sizes(last)
+        round_chunk_0(third)
+        round_to_pairs(third, 1, N_CHUNKS)
 
-        zw = keep.tile([P, S], U32, name="zw", align_bytes=64)
-        zs = keep.tile([P, S], U8, name="zs", align_bytes=64)
-        ow = keep.tile([P, S], I32, name="ow", align_bytes=64)
-        osc = keep.tile([P, S], U8, name="osc", align_bytes=64)
-        out_rows = out_0.rearrange("(p t) j -> p t j", t=PACK)
+        z_w = keep.tile([P, S], U32, name="z_w", align_bytes=64)
+        z_s = keep.tile([P, S], U8, name="z_s", align_bytes=64)
+        out_w = keep.tile([P, S], I32, name="out_w", align_bytes=64)
+        out_s = keep.tile([P, S], U8, name="out_s", align_bytes=64)
+        out_rows = out_0.rearrange("(p t) j -> p t j", t=SLOTS)
         out_words = as_words(out_1[0])
         chunks = [slice(CHUNK * c, CHUNK * (c + 1)) for c in range(N_CHUNKS)]
-        direct(t3, on_vector=True)
-        pair_up(t3, VEC_CHUNKS, N_CHUNKS)
-        for c in range(VEC_CHUNKS, N_CHUNKS):
-            weave(c, c + 1)
-        banks = []
+        round_chunk_0(last, on_vector=True)
+        round_to_pairs(last, VECTOR_CHUNKS, N_CHUNKS)
+        for c in range(VECTOR_CHUNKS, N_CHUNKS):
+            join_pairs(c)
+        scores = []
         for c, cols in enumerate(chunks):
-            if 0 < c < VEC_CHUNKS:
-                weave(c, c + 1, on_vector=True)
-            if c + 1 < VEC_CHUNKS:
-                pair_up(t3, c + 1, c + 2, on_vector=True)
-            nc.vector.quantize_mx(out=zw[:, cols].bitcast(FP8X4), scales=zs[:, cols],
-                                  in_=zb[:, cols, :].rearrange("p j t -> p (j t)"))
-            bank = psum.tile([P, PACK, CHUNK], F32, name=f"score{c}", tag=f"bank{c}")
-            banks.append(bank)
-            for t in range(PACK):
+            if 0 < c < VECTOR_CHUNKS:
+                join_pairs(c, on_vector=True)
+            if c + 1 < VECTOR_CHUNKS:
+                round_to_pairs(last, c + 1, c + 2, on_vector=True)
+            nc.vector.quantize_mx(out=z_w[:, cols].bitcast(FP8X4), scales=z_s[:, cols],
+                                  in_=z_bf[:, cols, :].rearrange("p j t -> p (j t)"))
+            score = psum.tile([P, SLOTS, CHUNK], F32, name=f"score{c}", tag=f"bank{c}")
+            scores.append(score)
+            for t in range(SLOTS):
                 rows = slice(P * t, P * (t + 1))
-                nc.tensor.matmul_mx(out=bank[:, t, :], lhsT=xcw[:, rows].bitcast(FP8X4), lhsT_scale=xcs[:, rows],
-                                    rhs=zw[:, cols].bitcast(FP8X4), rhs_scale=zs[:, cols], start=True, stop=True)
-        for pair in range(N_CHUNKS // 2):
-            ob = keep.tile([P, 2 * CHUNK, PACK], BF16, name=f"ob{pair}", align_bytes=64)
+                nc.tensor.matmul_mx(out=score[:, t, :], lhsT=cand_w[:, rows].bitcast(FP8X4), lhsT_scale=cand_s[:, rows],
+                                    rhs=z_w[:, cols].bitcast(FP8X4), rhs_scale=z_s[:, cols], start=True, stop=True)
+
+        for twin in range(N_CHUNKS // 2):
+            out_bf = keep.tile([P, 2 * CHUNK, SLOTS], BF16, name=f"out_bf{twin}", align_bytes=64)
             for i in range(2):
-                c = 2 * pair + i
-                res = keep.tile([P, PACK, CHUNK], F32, name=f"res{c}")
-                ob_c = ob[:, CHUNK * i : CHUNK * (i + 1), :].rearrange("p (c i) t -> p c t i", i=4)
+                c = 2 * twin + i
+                res = keep.tile([P, SLOTS, CHUNK], F32, name=f"res{c}")
+                rounded = out_bf[:, CHUNK * i : CHUNK * (i + 1), :].rearrange("p (c i) t -> p c t i", i=4)
                 if c == N_CHUNKS - 1:
-                    nc.scalar.activation(out=ob_c, in_=banks[c][:].rearrange("p t (c i) -> p c t i", i=4), func=ACT.Copy, scale=0.0625)
-                nc.scalar.activation(out=res[:], in_=banks[c][:], func=ACT.Copy, scale=0.0625)
+                    nc.scalar.activation(out=rounded, in_=scores[c][:].rearrange("p t (c i) -> p c t i", i=4),
+                                         func=ACT.Copy, scale=0.0625)
+                nc.scalar.activation(out=res[:], in_=scores[c][:], func=ACT.Copy, scale=0.0625)
                 nc.sync.dma_start(out=out_rows[:, :, chunks[c]], in_=res[:])
                 if c < N_CHUNKS - 1:
-                    nc.vector.tensor_copy(out=ob_c, in_=res[:].rearrange("p t (c i) -> p c t i", i=4))
-            both = slice(2 * CHUNK * pair, 2 * CHUNK * (pair + 1))
-            nc.vector.quantize_mx(out=ow[:, both].bitcast(FP8X4), scales=osc[:, both],
-                                  in_=ob[:].rearrange("p j t -> p (j t)"))
-            nc.sync.dma_start(out=out_words[:, both], in_=ow[:, both])
-        for q in range(QUADS):
-            eng = nc.sync if q % 2 == 0 else nc.scalar
-            eng.dma_start(out=out_2[0, q::4, :].bitcast(I32), in_=osc[q::32, :].bitcast(I32))
+                    nc.vector.tensor_copy(out=rounded, in_=res[:].rearrange("p t (c i) -> p c t i", i=4))
+            both = slice(2 * CHUNK * twin, 2 * CHUNK * (twin + 1))
+            nc.vector.quantize_mx(out=out_w[:, both].bitcast(FP8X4), scales=out_s[:, both],
+                                  in_=out_bf[:].rearrange("p j t -> p (j t)"))
+            nc.sync.dma_start(out=out_words[:, both], in_=out_w[:, both])
+        for r in range(SCALE_ROWS):
+            queue = nc.sync if r % 2 == 0 else nc.scalar
+            queue.dma_start(out=out_2[0, r::SCALE_ROWS, :].bitcast(I32), in_=out_s[r::QUADRANT, :].bitcast(I32))

from contextlib import ExitStack

import concourse.mybir as mybir

K, T, S, V, H, C = 512, 2048, 512, 256, 512, 512
FLOPS = 2 * K * H * S + 2 * K * C * S

F32 = mybir.dt.float32
BF16 = mybir.dt.bfloat16
I32 = mybir.dt.int32
U32 = mybir.dt.uint32
U16 = mybir.dt.uint16
U8 = mybir.dt.uint8
FP8X4 = mybir.dt.float8_e4m3fn_x4
ALU = mybir.AluOpType
ACT = mybir.ActivationFunctionType

P = 128
SLOTS = 4
QUADRANT = 32
SCALE_ROWS = 4
GROUP = 16
CHUNK = 128
N_CHUNKS = S // CHUNK
VECTOR_CHUNKS = 3
ORDER = (3, 0, 1, 2)


def as_words(dram_bytes):
    return dram_bytes.rearrange("p n t -> p (n t)").bitcast(I32)


def dealt(tile):
    return tile[:].rearrange("p (t m) -> p m t", t=SLOTS)


def list_columns(entries):
    return slice(entries.start // GROUP, entries.stop // GROUP)


def in_halves(n):
    return [slice(0, n // 2), slice(n // 2, n)]


def tile_picked_candhaar_none_po_kernel(
    tc, x_words, x_scales, w1_words, w1_scales, gs, offs, la, lb, cand, out_0, out_1, out_2
):
    nc = tc.nc
    first, second, third, last = ORDER
    with ExitStack() as ctx:
        keep = ctx.enter_context(tc.tile_pool(name="keep", bufs=1))
        psum = ctx.enter_context(tc.psum_pool(name="psum", bufs=1))

        offs_t = keep.tile([P, S // GROUP], U16, name="offs_t")
        cand_t = keep.tile([P, C // GROUP], U16, name="cand_t")
        la_t = keep.tile([P, V // GROUP], U16, name="la_t")
        lb_t = keep.tile([P, V // GROUP], U16, name="lb_t")
        x_w = keep.tile([P, T], I32, name="x_w", align_bytes=64)
        x_s = keep.tile([P, T], U8, name="x_s", align_bytes=64)
        w1_w = keep.tile([P, H], I32, name="w1_w", align_bytes=64)
        w1_s = keep.tile([P, H], U8, name="w1_s", align_bytes=64)
        gs_t = keep.tile([P, SLOTS], F32, name="gs_t")

        nc.vector.memset(x_s[:].bitcast(I32), 0)
        nc.vector.memset(w1_s[:].bitcast(I32), 0)
        for r in range(SCALE_ROWS):
            nc.sync.dma_start(out=x_s[r::QUADRANT, :].bitcast(I32), in_=x_scales[0, r::SCALE_ROWS, :].bitcast(I32))
        nc.sync.dma_start(offs_t[:], offs)
        nc.sync.dma_start(cand_t[:], cand)
        nc.sync.dma_start(la_t[:], la)
        nc.sync.dma_start(out=x_w[:], in_=as_words(x_words[0]))
        for r in range(SCALE_ROWS):
            nc.sync.dma_start(out=w1_s[r::QUADRANT, :].bitcast(I32), in_=w1_scales[0, r::SCALE_ROWS, :].bitcast(I32))
        nc.sync.dma_start(out=w1_w[:], in_=as_words(w1_words[0]))
        nc.sync.dma_start(lb_t[:], lb)
        nc.sync.dma_start(out=gs_t[:], in_=gs.rearrange("(p t) o -> p (t o)", t=SLOTS))

        w1_dealt_w = keep.tile([P, H], U32, name="w1_dealt_w", align_bytes=64)
        w1_dealt_s = keep.tile([P, H], U8, name="w1_dealt_s", align_bytes=64)
        w1_w_by_slot = w1_w[:].bitcast(U32).rearrange("p (m t) -> p m t", t=SLOTS)
        nc.scalar.copy(out=dealt(w1_dealt_w)[:, :, first], in_=w1_w_by_slot[:, :, first])
        nc.scalar.copy(out=dealt(w1_dealt_w)[:, :, :first], in_=w1_w_by_slot[:, :, :first])
        for t in ORDER:
            nc.gpsimd.tensor_copy(out=w1_dealt_s[:, P * t : P * (t + 1)], in_=w1_s[:, t::SLOTS])

        tok_w = keep.tile([P, S], U32, name="tok_w", align_bytes=64)
        tok_s = keep.tile([P, S], U8, name="tok_s", align_bytes=64)
        cand_w = keep.tile([P, C], U32, name="cand_w", align_bytes=64)
        cand_s = keep.tile([P, C], U8, name="cand_s", align_bytes=64)
        nc.vector.tensor_copy(tok_s[:], x_s[:].indirect(offs_t[:]))
        for half in in_halves(S):
            nc.vector.tensor_copy(tok_w[:, half], x_w[:].bitcast(U32).indirect(offs_t[:, list_columns(half)]))
        nc.vector.tensor_copy(dealt(cand_s), x_s[:].indirect(cand_t[:]))
        nc.vector.tensor_copy(dealt(cand_w), x_w[:].bitcast(U32).indirect(cand_t[:]))

        a = [keep.tile([P, V], F32, name=f"a{t}") for t in range(SLOTS)]
        b = [keep.tile([P, V], F32, name=f"b{t}") for t in range(SLOTS)]
        db = [keep.tile([P, V], F32, name=f"db{t}") for t in range(SLOTS)]
        d2 = [keep.tile([P, S], F32, name=f"d2_{t}") for t in range(SLOTS)]
        z_bf = keep.tile([P, S, SLOTS], BF16, name="z_bf", align_bytes=64)
        z_pairs = keep.tile([P, N_CHUNKS - 1, 2, CHUNK, 2], BF16, name="z_pairs", align_bytes=64)
        diff = {}

        def fetch(t):
            cols = slice(P * t, P * (t + 1))
            half_h = keep.tile([P, S], F32, name=f"half_h{t}")
            for i, toks in enumerate(in_halves(S) if t == first else [slice(0, S)]):
                h = psum.tile([P, toks.stop - toks.start], F32, name=f"h{t}{i}", tag=f"bank{t + SLOTS * i}")
                nc.tensor.matmul_mx(out=h[:], lhsT=w1_dealt_w[:, cols].bitcast(FP8X4), lhsT_scale=w1_dealt_s[:, cols],
                                    rhs=tok_w[:, toks].bitcast(FP8X4), rhs_scale=tok_s[:, toks], start=True, stop=True)
                nc.scalar.activation(out=half_h[:, toks], in_=h[:], func=ACT.Copy, scale=0.5)
            for pairs in in_halves(V) if t == first else [slice(0, V)]:
                at_la = half_h[:].indirect(la_t[:, list_columns(pairs)])
                at_lb = half_h[:].indirect(lb_t[:, list_columns(pairs)])
                nc.scalar.activation(out=a[t][:, pairs], in_=at_la, func=ACT.Copy)
                if pairs.stop < V:
                    nc.vector.tensor_copy(b[t][:, pairs], at_lb)
                else:
                    nc.scalar.activation(out=b[t][:, pairs], in_=at_lb, func=ACT.Copy)

        def put_means(t, pairs=slice(0, V)):
            nc.vector.tensor_tensor(d2[t][:].indirect(la_t[:, list_columns(pairs)]), a[t][:, pairs], b[t][:, pairs], ALU.add)

        def subtract(t):
            if t in (first, second):
                diff[t] = keep.tile([P, V], F32, name=f"diff{t}")
                nc.vector.tensor_tensor(diff[t][:], b[t][:], a[t][:], ALU.subtract)
            else:
                diff[t] = b[t]
                nc.gpsimd.tensor_tensor(diff[t][:], b[t][:], a[t][:], ALU.subtract)

        def take_size(t):
            nc.scalar.activation(out=db[t][:], in_=diff[t][:], func=ACT.Abs)

        def put_sizes(t):
            nc.vector.tensor_copy(d2[t][:].indirect(lb_t[:]), db[t][:])

        def times_gs(dst, src, t, on_vector):
            if on_vector:
                nc.vector.tensor_scalar(out=dst, in0=src, scalar1=gs_t[:, t : t + 1], scalar2=None, op0=ALU.mult)
            else:
                nc.scalar.activation(out=dst, in_=src, func=ACT.Copy, scale=gs_t[:, t : t + 1])

        def round_chunk_0(t, on_vector=False):
            times_gs(z_bf[:, :CHUNK, t], d2[t][:, :CHUNK], t, on_vector)

        def round_to_pairs(t, c0, c1, on_vector=False):
            src = d2[t][:, CHUNK * c0 : CHUNK * c1].rearrange("p (c j) -> p c j", j=CHUNK)
            times_gs(z_pairs[:, c0 - 1 : c1 - 1, t // 2, :, t % 2], src, t, on_vector)

        def join_pairs(c, on_vector=False):
            word = I32 if on_vector else U32
            dst = z_bf[:, CHUNK * c : CHUNK * (c + 1), :].bitcast(word)
            src = z_pairs[:, c - 1].rearrange("p w j e -> p w (j e)").bitcast(word).rearrange("p w j -> p j w")
            if on_vector:
                nc.vector.tensor_copy(out=dst, in_=src)
            else:
                nc.scalar.copy(out=dst, in_=src)

        fetch(first)
        put_means(first, in_halves(V)[0])
        subtract(first)
        take_size(first)
        put_means(first, in_halves(V)[1])
        put_sizes(first)
        fetch(second)
        put_means(second)
        subtract(second)
        fetch(third)
        take_size(second)
        put_means(third)
        subtract(third)
        fetch(last)
        round_chunk_0(first)
        round_to_pairs(first, 1, N_CHUNKS)
        take_size(third)
        put_sizes(second)
        put_means(last)
        subtract(last)
        round_chunk_0(second)
        round_to_pairs(second, 1, N_CHUNKS)
        take_size(last)
        put_sizes(third)
        put_sizes(last)
        round_chunk_0(third)
        round_to_pairs(third, 1, N_CHUNKS)

        z_w = keep.tile([P, S], U32, name="z_w", align_bytes=64)
        z_s = keep.tile([P, S], U8, name="z_s", align_bytes=64)
        out_w = keep.tile([P, S], I32, name="out_w", align_bytes=64)
        out_s = keep.tile([P, S], U8, name="out_s", align_bytes=64)
        out_rows = out_0.rearrange("(p t) j -> p t j", t=SLOTS)
        out_words = as_words(out_1[0])
        chunks = [slice(CHUNK * c, CHUNK * (c + 1)) for c in range(N_CHUNKS)]
        round_chunk_0(last, on_vector=True)
        round_to_pairs(last, VECTOR_CHUNKS, N_CHUNKS)
        for c in range(VECTOR_CHUNKS, N_CHUNKS):
            join_pairs(c)
        scores = []
        for c, cols in enumerate(chunks):
            if 0 < c < VECTOR_CHUNKS:
                join_pairs(c, on_vector=True)
            if c + 1 < VECTOR_CHUNKS:
                round_to_pairs(last, c + 1, c + 2, on_vector=True)
            nc.vector.quantize_mx(out=z_w[:, cols].bitcast(FP8X4), scales=z_s[:, cols],
                                  in_=z_bf[:, cols, :].rearrange("p j t -> p (j t)"))
            score = psum.tile([P, SLOTS, CHUNK], F32, name=f"score{c}", tag=f"bank{c}")
            scores.append(score)
            for t in range(SLOTS):
                rows = slice(P * t, P * (t + 1))
                nc.tensor.matmul_mx(out=score[:, t, :], lhsT=cand_w[:, rows].bitcast(FP8X4), lhsT_scale=cand_s[:, rows],
                                    rhs=z_w[:, cols].bitcast(FP8X4), rhs_scale=z_s[:, cols], start=True, stop=True)

        for twin in range(N_CHUNKS // 2):
            out_bf = keep.tile([P, 2 * CHUNK, SLOTS], BF16, name=f"out_bf{twin}", align_bytes=64)
            for i in range(2):
                c = 2 * twin + i
                res = keep.tile([P, SLOTS, CHUNK], F32, name=f"res{c}")
                rounded = out_bf[:, CHUNK * i : CHUNK * (i + 1), :].rearrange("p (c i) t -> p c t i", i=4)
                if c == N_CHUNKS - 1:
                    nc.scalar.activation(out=rounded, in_=scores[c][:].rearrange("p t (c i) -> p c t i", i=4),
                                         func=ACT.Copy, scale=0.0625)
                nc.scalar.activation(out=res[:], in_=scores[c][:], func=ACT.Copy, scale=0.0625)
                nc.sync.dma_start(out=out_rows[:, :, chunks[c]], in_=res[:])
                if c < N_CHUNKS - 1:
                    nc.vector.tensor_copy(out=rounded, in_=res[:].rearrange("p t (c i) -> p c t i", i=4))
            both = slice(2 * CHUNK * twin, 2 * CHUNK * (twin + 1))
            nc.vector.quantize_mx(out=out_w[:, both].bitcast(FP8X4), scales=out_s[:, both],
                                  in_=out_bf[:].rearrange("p j t -> p (j t)"))
            nc.sync.dma_start(out=out_words[:, both], in_=out_w[:, both])
        for r in range(SCALE_ROWS):
            queue = nc.sync if r % 2 == 0 else nc.scalar
            queue.dma_start(out=out_2[0, r::SCALE_ROWS, :].bitcast(I32), in_=out_s[r::QUADRANT, :].bitcast(I32))
